import numpy as np
import ml_dtypes


def mxq(x, axis, fmt="e4m3"):
    dtype, down = {"e4m3": (ml_dtypes.float8_e4m3fn, 7), "e5m2": (ml_dtypes.float8_e5m2, 14)}[fmt]
    v = np.moveaxis(np.asarray(x, np.float32).astype(ml_dtypes.bfloat16).astype(np.float64), axis, -1)
    blocks = v.reshape(v.shape[:-1] + (-1, 32))
    amax = np.abs(blocks).max(-1, keepdims=True)
    byte = np.maximum(np.where(amax > 0, np.frexp(amax)[1] - 1 + 127, 0) - down, 1)
    scale = np.exp2(byte - 127.0)
    codes = (blocks / scale).astype(np.float32).astype(dtype).astype(np.float64)
    return np.moveaxis((codes * scale).reshape(v.shape), -1, axis)


WIDE = False


def mx_kscale(k):
    if not WIDE:
        return np.ones(k)
    levels = np.array([10, -10, 5, -5, 0])
    if k % 512:
        return np.exp2(np.random.permutation(np.resize(levels, k // 32))).repeat(32)
    a = np.empty((k // 512, 16))
    for p in range(k // 512):
        a[p, :8] = np.random.permutation(np.resize(levels, 8))
        for g in range(8):
            far = levels[np.abs(levels - a[p, g]) >= 10]
            a[p, g + 8] = far[np.random.randint(len(far))]
    return np.exp2(a.ravel()).repeat(32)


BF16 = ml_dtypes.bfloat16


def bf(x):
    return np.asarray(x, np.float32).astype(BF16)


def f64(x):
    return np.asarray(x).astype(np.float64)


E2M1 = np.array([0.0, 0.5, 1.0, 1.5, 2.0, 3.0, 4.0, 6.0, -0.0, -0.5, -1.0, -1.5, -2.0, -3.0, -4.0, -6.0])


def pack_weight(w, fmt):
    k, n = w.shape
    w = f64(bf(w)).reshape(k // 32, 32, n)
    amax = np.abs(w).max(1)
    if fmt == "e4m3":
        byte = np.frexp(amax)[1] - 1 + 127 - 7
    else:
        mant, ex = np.frexp(amax / 6.0)
        byte = np.where(mant > 0.5, ex, ex - 1) + 127
    byte = np.clip(np.where(amax > 0, byte, 1), 1, 254)
    scaled = (w * np.exp2(127.0 - byte)[:, None, :]).reshape(k, n).astype(np.float32)
    by_word = np.ascontiguousarray(scaled.reshape(k // 512, 128, 4, n).transpose(0, 1, 3, 2))
    if fmt == "e4m3":
        words = by_word.astype(ml_dtypes.float8_e4m3fn).view(np.uint8)
    else:
        c = by_word.astype(ml_dtypes.float4_e2m1fn).view(np.uint8) & 0xF
        words = c[..., 0::2] | (c[..., 1::2] << 4)
    return np.ascontiguousarray(words), np.ascontiguousarray(byte.astype(np.uint8).reshape(k // 512, 16, n))


def unpack_weight(words, scales, fmt):
    g, p, n, _ = words.shape
    if fmt == "e4m3":
        vals = np.ascontiguousarray(words).view(ml_dtypes.float8_e4m3fn).astype(np.float64)
    else:
        nib = np.empty((g, p, n, 4), np.uint8)
        nib[..., 0::2] = words & 0xF
        nib[..., 1::2] = words >> 4
        vals = E2M1[nib]
    vals = vals * np.repeat(np.exp2(scales.astype(np.float64) - 127.0), 8, axis=1)[..., None]
    return vals.transpose(0, 1, 3, 2).reshape(g * 512, n)
def pack4(w):
    words, scales = pack_weight(w, "e2m1")
    return words.reshape(words.shape[0], 128, -1), scales


def unpack4(words, scales):
    return unpack_weight(words.reshape(words.shape[0], 128, -1, 2), scales, "e2m1")


E4M3FN = np.array([(-1.0 if i & 128 else 1.0) * ((1.0 + (i & 7) / 8.0) * 2.0 ** (((i >> 3) & 15) - 7) if i & 120 else (i & 7) * 2.0 ** -9) for i in range(256)])


def e4m3fn_bytes(y):
    return np.clip(np.asarray(y, np.float64), -448.0, 448.0).astype(np.float32).astype(ml_dtypes.float8_e4m3fn).view(np.uint8)


def e4m3fn_values(b):
    return E4M3FN[b]

def planes(Y):
    n, m = Y.shape
    b = f64(bf(Y)).reshape(n // 32, 32, m)
    amax = np.abs(b).max(1)
    byte = np.clip(np.where(amax > 0, np.frexp(amax)[1] - 1 + 127 - 7, 1), 1, 254)
    codes = (b * np.exp2(127.0 - byte)[:, None, :]).reshape(n, m).astype(np.float32).astype(ml_dtypes.float8_e4m3fn).view(np.uint8)
    words = codes.reshape(n // 512, 128, 4, m).transpose(0, 1, 3, 2)
    return np.ascontiguousarray(words), np.ascontiguousarray(byte.astype(np.uint8).reshape(n // 512, 16, m))


G, T, K, F, P, B = 4, 256, 1024, 1536, 512, 128

def setup_inputs():
    n = np.random.standard_normal
    s = mx_kscale(K)
    t = mx_kscale(F)
    x = n((G, T, K)) * np.exp(0.3 * n((G, T, 1))) * s
    x_scale = (np.abs(x).reshape(G, T, K // B, B).max(axis=3) / 448.0).astype(np.float32)
    x_bytes = e4m3fn_bytes(x / np.repeat(f64(x_scale), B, axis=2))
    u = n((G, K, F)) / np.sqrt(K) / s[:, None] * t
    v = n((G, K, F)) / np.sqrt(K) / s[:, None] * t
    r = n((G, F, P)) / np.sqrt(F) / t[:, None]
    u_words, u_scales = pack4(u.reshape(G * K, F))
    v_words, v_scales = pack4(v.reshape(G * K, F))
    r_words, r_scales = pack4(r.reshape(G * F, P))
    return {"X_bytes": x_bytes, "X_scale": x_scale,
            "U_words": u_words, "U_scales": u_scales,
            "V_words": v_words, "V_scales": v_scales,
            "R_words": r_words, "R_scales": r_scales,
            "u_bias": bf(0.4 * n((G, F)) * t), "v_bias": bf(0.4 * n((G, F)) * t),
            "score_bias": bf(0.4 * n((G, P))), "score_gain": bf(np.exp(0.8 * n((G, P))))}

def reference(X_bytes, X_scale, U_words, U_scales, V_words, V_scales, R_words, R_scales,
              u_bias, v_bias, score_bias, score_gain):
    X = e4m3fn_values(X_bytes) * np.repeat(f64(X_scale), B, axis=2)
    U = unpack4(U_words, U_scales).reshape(G, K, F)
    V = unpack4(V_words, V_scales).reshape(G, K, F)
    R = unpack4(R_words, R_scales).reshape(G, F, P)
    Xq = mxq(X, 2, "e4m3")
    a = (Xq @ U) + f64(u_bias)[:, None, :]
    b = (Xq @ V) + f64(v_bias)[:, None, :]
    H = np.maximum(a, b)
    z = mxq(H, 2, "e4m3") @ R
    y = (z + f64(score_bias)[:, None, :]) * f64(score_gain)[:, None, :]
    Y = y.transpose(2, 0, 1).reshape(P, G * T)
    words, scales = planes(Y)
    return y, words, scales

@@ -1,0 +1,438 @@
+from contextlib import ExitStack
+
+import concourse.mybir as mybir
+from concourse.masks import make_identity
+
+G, T, K, F, NS = 4, 256, 1024, 1536, 512
+FLOPS = 2 * G * T * (2 * K * F + F * NS)
+
+F32 = mybir.dt.float32
+BF16 = mybir.dt.bfloat16
+I32 = mybir.dt.int32
+U32 = mybir.dt.uint32
+U8 = mybir.dt.uint8
+FP8 = mybir.dt.float8_e4m3fn
+FP8X4 = mybir.dt.float8_e4m3fn_x4
+FP4X4 = mybir.dt.float4_e2m1fn_x4
+ALU = mybir.AluOpType
+ACT = mybir.ActivationFunctionType
+
+P = 128
+KP = K // 512
+FP = F // 512
+NCH = G * FP
+MODES = "CBB" * 8
+WIDEN = "VVSVSVSV"
+GAIN = "VVVVVVVV"
+LAG1 = 2
+LAG2 = 4
+LAGB = 2
+RUN = 2
+XLEAD = 4
+WLEAD = 3
+ZLAG = 2
+YLAG = 3
+UNITS = ([(0, h, g) for g in range(FP) for h in range(2)]
+         + [(d, h, g) for d in range(1, G) for h in range(2) for g in range(FP)])
+NEED = sorted(set(FP * d + g for i, (d, h, g) in enumerate(UNITS) if MODES[i] == "B"))
+
+
+def tile_dialect_maxout_phoneme_scores_b12_kernel(
+    tc, X_bytes, X_scale, U_words, U_scales, V_words, V_scales, R_words, R_scales,
+    u_bias, v_bias, score_bias, score_gain, out_0, out_1, out_2,
+):
+    nc = tc.nc
+    with ExitStack() as ctx:
+        keep = ctx.enter_context(tc.tile_pool(name="keep", bufs=1))
+        work = ctx.enter_context(tc.tile_pool(name="work", bufs=2))
+        psum = ctx.enter_context(tc.psum_pool(name="psum", bufs=1))
+        ctx.enter_context(tc.manual_schedule(engines={mybir.EngineType.PE, mybir.EngineType.SP}))
+
+        def kept(name, shape, dtype):
+            return keep.tile(shape, dtype, name=name, align_bytes=64)
+
+        ident_f = kept("ident_f", [P, P], F32)
+        ident_b = kept("ident_b", [P, P], BF16)
+        bias_rows = kept("bias_rows", [P, P], BF16)
+        bias_cols = kept("bias_cols", [P, 96], F32)
+        warm = kept("warm", [P, 8], F32)
+        x_scale = kept("x_scale", [P, 2 * G, 8], F32)
+        x_bytes = [kept("x_bytes%d" % d, [P, 2, K], U8) for d in range(G)]
+        w0 = [[kept("w0_%d_%d" % (m, g), [P, KP, 1024], U8) for g in range(FP)] for m in range(2)]
+        wd = [[None] + [kept("w%d_%d" % (d, m), [P, KP, 2 * F], U8) for d in range(1, G)] for m in range(2)]
+        ws0 = [kept("ws0_%d" % m, [P, KP * F], U8) for m in range(2)]
+        ws1 = [kept("ws1_%d" % m, [P, KP * F], U8) for m in range(2)]
+        wsr = [kept("wsr_%d" % m, [P, 2 * KP * F], U8) for m in range(2)]
+        spread = {(m, n): kept("spread%d_%d" % (m, n), [P, 512], BF16)
+                  for n in NEED for m in range(2)}
+        bias_in = (u_bias, v_bias)
+        r_words = [kept("r_words%d" % d, [P, FP, 2 * NS], U8) for d in range(G)]
+        r_scales = kept("r_scales", [P, G * FP * NS], U8)
+        s_bias = kept("s_bias", [P, G * NS], BF16)
+        s_gain = kept("s_gain", [P, G * NS], BF16)
+        y_scales = [kept("y_scales%d" % i, [P, w], U8) for i, w in enumerate((7 * P, P))]
+        y_words = [kept("y_words%d" % i, [P, T], U32) for i in range(G)]
+        words_in = (U_words, V_words)
+        scales_in = (U_scales, V_scales)
+
+        def load_scales(tile, src, n):
+            rows = src.rearrange("g (q r) n -> r q g n", r=4)
+            for r in range(4):
+                nc.sync.dma_start(
+                    out=tile[r:P:32, :].bitcast(I32).rearrange("q (g n) -> q g n", n=n // 4),
+                    in_=rows[r].bitcast(I32))
+
+        def load_x(d):
+            nc.sync.dma_start(out=x_bytes[d][:], in_=X_bytes[d].rearrange("(h p) k -> p h k", p=P))
+
+        def load_w0(m, g):
+            src = words_in[m][0:KP].rearrange("g p n -> p g n")[:, :, 1024 * g:1024 * (g + 1)]
+            nc.sync.dma_start(out=w0[m][g][:].bitcast(I32), in_=src.bitcast(I32))
+
+        def load_w(m, d):
+            src = words_in[m][KP * d:KP * (d + 1)].rearrange("g p n -> p g n")
+            nc.sync.dma_start(out=wd[m][d][:].bitcast(I32), in_=src.bitcast(I32))
+
+        def load_r(d):
+            src = R_words[FP * d:FP * (d + 1)].rearrange("g p n -> p g n")
+            nc.sync.dma_start(out=r_words[d][:].bitcast(I32), in_=src.bitcast(I32))
+
+        def load_spread(n):
+            if n in NEED:
+                d, g = divmod(n, FP)
+                for m in range(2):
+                    nc.sync.dma_start(out=spread[m, n][:],
+                                      in_=bias_in[m][d, 512 * g:512 * (g + 1)].partition_broadcast(P))
+
+        def w_operand(m, d, g, kp, c0, width):
+            col = 512 * g + c0
+            if d == 0:
+                words = w0[m][g][:, kp, 2 * c0:2 * (c0 + width)]
+            else:
+                words = wd[m][d][:, kp, 2 * col:2 * (col + width)]
+            plane = (ws0, ws1, wsr, wsr)[d][m]
+            at = (max(d - 2, 0) * KP + kp) * F + col
+            return words.bitcast(FP4X4), plane[:, at:at + width]
+
+        nc.vector.memset(ws0[0][:].bitcast(I32), 0)
+        nc.vector.memset(ws0[1][:].bitcast(I32), 0)
+        nc.vector.memset(bias_rows[96:P, :], 0.0)
+        nc.vector.memset(warm[:], 0.0)
+        nc.vector.memset(ws1[0][:].bitcast(I32), 0)
+        nc.vector.memset(ws1[1][:].bitcast(I32), 0)
+        make_identity(nc, ident_f[:])
+        make_identity(nc, ident_b[:])
+        load_x(0)
+        nc.sync.dma_start(out=x_scale[:], in_=X_scale.rearrange("d (h p) j -> p (d h) j", p=P))
+        nc.scalar.dma_start(out=bias_rows[0:48, :], in_=u_bias.rearrange("d (j c) -> (d j) c", c=P))
+        nc.scalar.dma_start(out=bias_rows[48:96, :], in_=v_bias.rearrange("d (j c) -> (d j) c", c=P))
+        nc.scalar.activation(out=warm[:], in_=warm[:], func=ACT.Identity)
+        load_scales(ws0[0], U_scales[0:KP], F)
+        load_w0(0, 0)
+        load_w0(1, 0)
+        load_scales(ws0[1], V_scales[0:KP], F)
+        load_spread(0)
+        for g in range(1, FP):
+            load_w0(0, g)
+            load_w0(1, g)
+            load_spread(g)
+        load_x(1)
+
+        xw, xq, xs, hn, hs, hq, hsc, yf, yb, zb = {}, {}, {}, {}, {}, {}, {}, {}, {}, {}
+        bank, staged = {}, {}
+        done = set()
+
+        def aux():
+            return psum.tile([P, 512], F32, name="aux", tag="aux", bufs=2)
+
+        def sb(name, cols, dtype, bufs):
+            return work.tile([P, cols], dtype, name=name, tag=name, bufs=bufs, align_bytes=64)
+
+        def widen(i, part):
+            d, h = divmod(i, 2)
+            if part == 0:
+                xw[i] = sb("xw", K, BF16, 2)
+                if WIDEN[i] == "S":
+                    staged["plain"] = sb("x_plain", K, BF16, 2)
+            t = xw[i]
+            if WIDEN[i] == "S":
+                plain = staged["plain"]
+                for blk in range(4 * part, 4 * part + 4):
+                    nc.scalar.activation(out=plain[:, P * blk:P * (blk + 1)], func=ACT.Copy,
+                                         in_=x_bytes[d][:, h, P * blk:P * (blk + 1)].bitcast(FP8),
+                                         scale=x_scale[:, i, blk:blk + 1])
+                cols = slice(512 * part, 512 * (part + 1))
+                nc.scalar.copy(out=t[:, cols].bitcast(F32).rearrange("p (u c) -> p u c", u=2),
+                               in_=plain[:, cols].bitcast(F32).rearrange("p (c u) -> p u c", u=2))
+                return
+            dst = t[:].rearrange("p (g u b a e) -> p g b a u e", g=KP, u=2, b=4, e=2)
+            for blk in range(4 * part, 4 * part + 4):
+                src = x_bytes[d][:, h, P * blk:P * (blk + 1)].bitcast(FP8)
+                nc.vector.tensor_scalar(
+                    out=dst[:, blk // 4, blk % 4], in0=src.rearrange("p (a u e) -> p a u e", u=2, e=2),
+                    scalar1=x_scale[:, i, blk:blk + 1], scalar2=None, op0=ALU.mult)
+
+        def turn_words(dst, src):
+            words = src.bitcast(F32)
+            for i in range(words.shape[1] // P):
+                nc.tensor.transpose(dst[:, P * i:P * (i + 1)], words[:, P * i:P * (i + 1)], ident_f[:])
+
+        def interleave_out(name, src, bufs):
+            t = sb(name, 2 * src.shape[1], BF16, bufs)
+            nc.scalar.copy(out=t[:].bitcast(F32).rearrange("p (i c u) -> p i c u", c=P, u=2),
+                           in_=src.rearrange("p (i u c) -> p i c u", c=P, u=2))
+            return t
+
+        def quant(src, codes, scales):
+            nc.vector.quantize_mx(out=codes.bitcast(FP8X4), scales=scales, in_=src[:])
+
+        def turn_x(i):
+            bank["x", i] = aux()
+            turn_words(bank["x", i], xw[i][:])
+
+        def exit_x(i):
+            staged["x", i] = interleave_out("x_in", bank["x", i][:], 2)
+
+        def quant_x(i):
+            xq[i] = sb("xq", KP * P, U32, 4)
+            xs[i] = sb("xs", KP * P, U8, 4)
+            quant(staged["x", i], xq[i][:], xs[i][:])
+
+        def stage1(s):
+            d, h, g = UNITS[s]
+            i = 2 * d + h
+            n = FP * d + g
+            acc = []
+            for m in range(2):
+                b = psum.tile([P, 512], F32, name="acc%d" % m, tag="acc%d" % m, bufs=2)
+                acc.append(b)
+                for j in range(4 if MODES[s] == "C" else 1):
+                    for kp in range(KP):
+                        xc = xq[i][:, P * kp:P * (kp + 1)].bitcast(FP8X4)
+                        xp = xs[i][:, P * kp:P * (kp + 1)]
+                        if MODES[s] == "C":
+                            ww, wsc = w_operand(m, d, g, kp, P * j, P)
+                            nc.tensor.matmul_mx(out=b[:, P * j:P * (j + 1)], lhsT=ww, lhsT_scale=wsc, rhs=xc,
+                                                rhs_scale=xp, start=(kp == 0), stop=(kp == KP - 1))
+                        else:
+                            ww, wsc = w_operand(m, d, g, kp, 0, 512)
+                            nc.tensor.matmul_mx(out=b[:], lhsT=xc, lhsT_scale=xp, rhs=ww, rhs_scale=wsc,
+                                                start=(kp == 0), stop=(kp == KP - 1))
+            bank["acc", s] = acc
+
+        def maxout(s):
+            d, h, g = UNITS[s]
+            n = FP * d + g
+            acc = bank["acc", s]
+            if MODES[s] == "C":
+                hn[s] = sb("hn", 512, BF16, 4)
+                tmp = [sb("a_tmp", P, F32, 8) for j in range(4)]
+                for j in range(4):
+                    nc.scalar.activation(out=tmp[j][:], in_=acc[0][:, P * j:P * (j + 1)], func=ACT.Identity,
+                                         bias=bias_cols[:, 4 * n + j:4 * n + j + 1])
+                for j in range(4):
+                    nc.vector.scalar_tensor_tensor(
+                        out=hn[s][:, P * j:P * (j + 1)], in0=acc[1][:, P * j:P * (j + 1)],
+                        scalar=bias_cols[:, 48 + 4 * n + j:49 + 4 * n + j], in1=tmp[j][:], op0=ALU.add, op1=ALU.max)
+                return
+            part = [sb("part", 512, BF16, 4) for m in range(2)]
+            staged["part", s] = part
+            for m in range(2):
+                nc.vector.tensor_tensor(
+                    out=part[m][:].rearrange("p (u c e) -> p u c e", u=2, e=2),
+                    in0=acc[m][:].rearrange("p (c u e) -> p u c e", u=2, e=2),
+                    in1=spread[m, n][:].rearrange("p (c u e) -> p u c e", u=2, e=2), op=ALU.add)
+
+        def larger(s):
+            hs[s] = sb("hs", 512, BF16, 6)
+            part = staged["part", s]
+            nc.vector.tensor_tensor(out=hs[s][:], in0=part[0][:], in1=part[1][:], op=ALU.max)
+
+        def turn_h1(s, at):
+            for j in range(4):
+                nc.tensor.transpose(bank["h1"][:, 512 * at + P * j:512 * at + P * (j + 1)],
+                                    hn[s][:, P * j:P * (j + 1)], ident_b[:])
+
+        def exit_h1(s, at):
+            hs[s] = sb("hs", 512, BF16, 6)
+            nc.scalar.copy(out=hs[s][:].bitcast(F32).rearrange("p (u c) -> p u c", u=2),
+                           in_=bank["h1"][:, 512 * at:512 * (at + 1)].bitcast(F32).rearrange("p (c u) -> p u c", u=2))
+
+        def quant_h(group):
+            src = staged["h"]
+            codes = sb("hq", P * len(group), U32, 5)
+            plane = sb("hsc", P * len(group), U8, 5)
+            quant(src, codes[:], plane[:])
+            for at, s in enumerate(group):
+                hq[UNITS[s]] = (codes[:, P * at:P * (at + 1)].bitcast(FP8X4), plane[:, P * at:P * (at + 1)])
+
+        def stage2(i, passes):
+            d, h = divmod(i, 2)
+            if passes[0] == 0:
+                bank["z", i] = aux()
+            for g in passes:
+                n = FP * d + g
+                nc.tensor.matmul_mx(
+                    out=bank["z", i][:], lhsT=hq[d, h, g][0], lhsT_scale=hq[d, h, g][1],
+                    rhs=r_words[d][:, g, :].bitcast(FP4X4), rhs_scale=r_scales[:, NS * n:NS * (n + 1)],
+                    start=(g == 0), stop=(g == FP - 1))
+
+        def add_bias(i):
+            zb[i] = sb("zb", NS, F32, 2)
+            nc.vector.tensor_tensor(out=zb[i][:], in0=bank["z", i][:],
+                                    in1=s_bias[:, NS * (i // 2):NS * (i // 2 + 1)], op=ALU.add)
+
+        def gain(i):
+            d, h = divmod(i, 2)
+            yf[i] = sb("yf", NS, F32, 8)
+            eng = nc.vector if GAIN[i] == "V" else nc.gpsimd
+            eng.tensor_tensor(out=yf[i][:], in0=zb[i][:], in1=s_gain[:, NS * d:NS * (d + 1)], op=ALU.mult)
+            nc.sync.dma_start(out=out_0[d, P * h:P * (h + 1), :], in_=yf[i][:])
+
+        def round_y(i):
+            yb[i] = sb("yb", NS, BF16, 2)
+            nc.scalar.copy(out=yb[i][:].rearrange("p (u c e) -> p u c e", u=2, e=2),
+                           in_=yf[i][:].rearrange("p (c u e) -> p u c e", u=2, e=2))
+
+        def turn_y(i):
+            bank["y", i] = aux()
+            turn_words(bank["y", i], yb[i][:])
+
+        def exit_y(i):
+            staged["y", i] = interleave_out("y_in", bank["y", i][:, 0:T], 2)
+
+        def quant_y(i):
+            d, h = divmod(i, 2)
+            done.add(i)
+            assert i < 6 or len(done) == i + 1
+            quant(staged["y", i], y_words[d][:, P * h:P * (h + 1)], y_scales[i // 7][:, P * (i % 7):P * (i % 7 + 1)])
+            rows = out_1[0].rearrange("p m t -> p (m t)").bitcast(I32)
+            if i >= 6:
+                nc.sync.dma_start(out=rows[:, P * i:P * (i + 1)], in_=y_words[d][:, P * h:P * (h + 1)].bitcast(I32))
+            elif 2 * d + 1 - h in done:
+                nc.sync.dma_start(out=rows[:, T * d:T * (d + 1)], in_=y_words[d][:].bitcast(I32))
+            if i >= 6:
+                cols = slice(0, 7 * P) if i == 6 else slice(7 * P, 8 * P)
+                for q in range(4):
+                    eng = nc.scalar if (i == 7 and q % 2) else nc.sync
+                    eng.dma_start(out=out_2[0, 4 * q:4 * q + 4, cols].bitcast(I32),
+                                  in_=y_scales[i // 7][32 * q:32 * q + 4, :].bitcast(I32))
+
+        for i in range(2):
+            widen(i, 0)
+            widen(i, 1)
+        turn_x(0)
+        exit_x(0)
+        quant_x(0)
+        turn_x(1)
+        exit_x(1)
+        bt = psum.tile([P, 1024], BF16, name="h1", tag="h1")
+        nc.tensor.transpose(bt[:, 0:P], bias_rows[:], ident_b[:])
+        nc.scalar.copy(out=bias_cols[:], in_=bt[:, 0:96])
+        quant_x(1)
+        nc.vector.memset(r_scales[:].bitcast(I32), 0)
+        nc.vector.memset(wsr[0][:].bitcast(I32), 0)
+        nc.vector.memset(wsr[1][:].bitcast(I32), 0)
+        load_scales(ws1[0], U_scales[KP:2 * KP], F)
+        load_scales(ws1[1], V_scales[KP:2 * KP], F)
+        load_w(0, 1)
+        load_w(1, 1)
+        for n in range(3, 6):
+            load_spread(n)
+        load_x(2)
+        load_scales(r_scales, R_scales, NS)
+        load_r(0)
+        nc.sync.dma_start(out=s_bias[:], in_=score_bias.rearrange("d n -> (d n)").partition_broadcast(P))
+        nc.sync.dma_start(out=s_gain[:], in_=score_gain.rearrange("d n -> (d n)").partition_broadcast(P))
+        load_scales(wsr[0], U_scales[2 * KP:], F)
+        load_scales(wsr[1], V_scales[2 * KP:], F)
+        for d in range(2, G):
+            load_w(0, d)
+            load_w(1, d)
+            for n in range(FP * d, FP * (d + 1)):
+                load_spread(n)
+            if d + 1 < G:
+                load_x(d + 1)
+            load_r(d - 1)
+        load_r(G - 1)
+
+
+        last = len(UNITS) - 1
+        start_of = {2 * d + h: min(s for s, u in enumerate(UNITS) if u[:2] == (d, h)) for d in range(G) for h in range(2)}
+        todo = {}
+
+        def at(step, slot, fn, *args):
+            todo.setdefault((step, slot), []).append((fn, args))
+
+        def run(step, slot):
+            for fn, args in todo.get((step, slot), []):
+                fn(*args)
+
+        def is_run(step):
+            return step >= last or step % RUN == RUN - 1
+
+        def run_from(step):
+            while not is_run(step):
+                step = step + 1
+            return step
+
+        wait1, wait2 = [], []
+        left = {i: FP for i in range(2 * G)}
+        for i in range(2, 2 * G):
+            r = run_from(max(start_of[i] - XLEAD, 1))
+            at(max(r - WLEAD, 0), "late", widen, i, 0)
+            at(max(r - WLEAD, 0) + 1, "late", widen, i, 1)
+            at(r, "turn", turn_x, i)
+            at(r, "exit", exit_x, i)
+            at(r + 1, "early", quant_x, i)
+        for s in range(last + 12):
+            if s <= last:
+                stage1(s)
+            run(s, "mx")
+            run(s, "early")
+            if s <= last:
+                maxout(s)
+                if MODES[s] == "C":
+                    wait1.append((s, s + LAG1 - (s >= last)))
+                elif s < last:
+                    at(s + 1, "early", larger, s)
+                    wait2.append((s, s + LAGB - (s + 1 >= last)))
+                else:
+                    larger(s)
+                    wait2.append((s, s + 1))
+            run(s, "late")
+            if not is_run(s):
+                continue
+            first = [u for u, due in wait1 if due <= s][:2]
+            second = [u for u, due in sorted(wait2) if due <= s][:2]
+            wait1 = [w for w in wait1 if w[0] not in first]
+            wait2 = [w for w in wait2 if w[0] not in second]
+            if second:
+                bank["h2"] = psum.tile([P, 512], F32, name="h2", tag="h2")
+                for k, u in enumerate(second):
+                    turn_words(bank["h2"][:, T * k:T * (k + 1)], hs[u][:])
+            run(s, "turn")
+            if first:
+                bank["h1"] = psum.tile([P, 1024], BF16, name="h1", tag="h1")
+                for k, u in enumerate(first):
+                    turn_h1(u, k)
+            if second:
+                staged["h"] = interleave_out("h_in", bank["h2"][:, 0:T * len(second)], 2)
+                at(s + 1, "early", quant_h, second)
+                for u in second:
+                    i = 2 * UNITS[u][0] + UNITS[u][1]
+                    left[i] = left[i] - 1
+                    if left[i] == 0:
+                        z = s + 1 + (ZLAG if s < last else 1)
+                        at(z, "mx", stage2, i, list(range(FP)))
+                        at(z, "late", add_bias, i)
+                        at(z + 1, "early", gain, i)
+                        at(z + 1, "late", round_y, i)
+                        r = run_from(z + (YLAG if z + YLAG <= last else 1))
+                        at(r, "turn", turn_y, i)
+                        at(r, "exit", exit_y, i)
+                        at(r + 1, "early", quant_y, i)
+            run(s, "exit")
+            for k, u in enumerate(first):
+                exit_h1(u, k)
+                wait2.append((u, s + 1))

@@ -21,8 +21,8 @@ P = 128
 KP = K // 512
 FP = F // 512
 NCH = G * FP
-MODES = "CBB" * 8
-WIDEN = "VVSVSVSV"
+MODES = "C" * 24
+WIDEN = "V" * 8
 GAIN = "VVVVVVVV"
 LAG1 = 2
 LAG2 = 4
@@ -31,6 +31,14 @@ RUN = 2
 XLEAD = 4
 WLEAD = 3
 ZLAG = 2
+TAIL = 22
+ZT = 1
+YT = 2
+SC2 = 2
+SC3 = 4
+YCAP = 2
+SPX = "VSSS"
+SLEAD = 2
 YLAG = 3
 UNITS = ([(0, h, g) for g in range(FP) for h in range(2)]
          + [(d, h, g) for d in range(1, G) for h in range(2) for g in range(FP)])
@@ -46,7 +54,7 @@ def tile_dialect_maxout_phoneme_scores_b12_kernel(
         keep = ctx.enter_context(tc.tile_pool(name="keep", bufs=1))
         work = ctx.enter_context(tc.tile_pool(name="work", bufs=2))
         psum = ctx.enter_context(tc.psum_pool(name="psum", bufs=1))
-        ctx.enter_context(tc.manual_schedule(engines={mybir.EngineType.PE, mybir.EngineType.SP}))
+        ctx.enter_context(tc.manual_schedule())
 
         def kept(name, shape, dtype):
             return keep.tile(shape, dtype, name=name, align_bytes=64)
@@ -63,13 +71,10 @@ def tile_dialect_maxout_phoneme_scores_b12_kernel(
         ws0 = [kept("ws0_%d" % m, [P, KP * F], U8) for m in range(2)]
         ws1 = [kept("ws1_%d" % m, [P, KP * F], U8) for m in range(2)]
         wsr = [kept("wsr_%d" % m, [P, 2 * KP * F], U8) for m in range(2)]
-        spread = {(m, n): kept("spread%d_%d" % (m, n), [P, 512], BF16)
-                  for n in NEED for m in range(2)}
-        bias_in = (u_bias, v_bias)
+        spread = {}
         r_words = [kept("r_words%d" % d, [P, FP, 2 * NS], U8) for d in range(G)]
         r_scales = kept("r_scales", [P, G * FP * NS], U8)
-        s_bias = kept("s_bias", [P, G * NS], BF16)
-        s_gain = kept("s_gain", [P, G * NS], BF16)
+        score = [kept("score%d" % d, [P, 2 * NS], BF16) for d in range(G)]
         y_scales = [kept("y_scales%d" % i, [P, w], U8) for i, w in enumerate((7 * P, P))]
         y_words = [kept("y_words%d" % i, [P, T], U32) for i in range(G)]
         words_in = (U_words, V_words)
@@ -97,13 +102,6 @@ def tile_dialect_maxout_phoneme_scores_b12_kernel(
             src = R_words[FP * d:FP * (d + 1)].rearrange("g p n -> p g n")
             nc.sync.dma_start(out=r_words[d][:].bitcast(I32), in_=src.bitcast(I32))
 
-        def load_spread(n):
-            if n in NEED:
-                d, g = divmod(n, FP)
-                for m in range(2):
-                    nc.sync.dma_start(out=spread[m, n][:],
-                                      in_=bias_in[m][d, 512 * g:512 * (g + 1)].partition_broadcast(P))
-
         def w_operand(m, d, g, kp, c0, width):
             col = 512 * g + c0
             if d == 0:
@@ -116,7 +114,6 @@ def tile_dialect_maxout_phoneme_scores_b12_kernel(
 
         nc.vector.memset(ws0[0][:].bitcast(I32), 0)
         nc.vector.memset(ws0[1][:].bitcast(I32), 0)
-        nc.vector.memset(bias_rows[96:P, :], 0.0)
         nc.vector.memset(warm[:], 0.0)
         nc.vector.memset(ws1[0][:].bitcast(I32), 0)
         nc.vector.memset(ws1[1][:].bitcast(I32), 0)
@@ -126,16 +123,16 @@ def tile_dialect_maxout_phoneme_scores_b12_kernel(
         nc.sync.dma_start(out=x_scale[:], in_=X_scale.rearrange("d (h p) j -> p (d h) j", p=P))
         nc.scalar.dma_start(out=bias_rows[0:48, :], in_=u_bias.rearrange("d (j c) -> (d j) c", c=P))
         nc.scalar.dma_start(out=bias_rows[48:96, :], in_=v_bias.rearrange("d (j c) -> (d j) c", c=P))
+        nc.scalar.dma_start(out=bias_rows[96:112, :], in_=score_bias.rearrange("d (j c) -> (d j) c", c=P))
+        nc.scalar.dma_start(out=bias_rows[112:P, :], in_=score_gain.rearrange("d (j c) -> (d j) c", c=P))
         nc.scalar.activation(out=warm[:], in_=warm[:], func=ACT.Identity)
-        load_scales(ws0[0], U_scales[0:KP], F)
         load_w0(0, 0)
+        load_scales(ws0[0], U_scales[0:KP], F)
         load_w0(1, 0)
         load_scales(ws0[1], V_scales[0:KP], F)
-        load_spread(0)
         for g in range(1, FP):
             load_w0(0, g)
             load_w0(1, g)
-            load_spread(g)
         load_x(1)
 
         xw, xq, xs, hn, hs, hq, hsc, yf, yb, zb = {}, {}, {}, {}, {}, {}, {}, {}, {}, {}
@@ -185,6 +182,27 @@ def tile_dialect_maxout_phoneme_scores_b12_kernel(
 
         def quant(src, codes, scales):
             nc.vector.quantize_mx(out=codes.bitcast(FP8X4), scales=scales, in_=src[:])
+
+        def spread_rows(tag, bufs, first, second):
+            b = psum.tile([P, 1024], BF16, name=tag, tag=tag, bufs=bufs)
+            for k, r in enumerate(list(range(first, first + 4)) + list(range(second, second + 4))):
+                nc.tensor.matmul(b[:, P * k:P * (k + 1)], lhsT=ident_b[:, r:r + 1].to_broadcast([P, P]),
+                                 rhs=bias_rows[:], start=True, stop=True)
+            return b
+
+        def copy_out(which, dst, src):
+            if which == "S":
+                nc.scalar.copy(out=dst, in_=src)
+            else:
+                nc.vector.tensor_copy(out=dst, in_=src)
+
+        def spread_unit(n):
+            b = spread_rows("aux", 2, 4 * n, 48 + 4 * n)
+            spread[n] = sb("spread", 1024, BF16, 4)
+            nc.scalar.copy(out=spread[n][:], in_=b[:])
+
+        def spread_score(d):
+            copy_out(SPX[d], score[d][:], spread_rows("aux", 2, 96 + 4 * d, 112 + 4 * d)[:])
 
         def turn_x(i):
             bank["x", i] = aux()
@@ -238,15 +256,16 @@ def tile_dialect_maxout_phoneme_scores_b12_kernel(
             part = [sb("part", 512, BF16, 4) for m in range(2)]
             staged["part", s] = part
             for m in range(2):
-                nc.vector.tensor_tensor(
-                    out=part[m][:].rearrange("p (u c e) -> p u c e", u=2, e=2),
-                    in0=acc[m][:].rearrange("p (c u e) -> p u c e", u=2, e=2),
-                    in1=spread[m, n][:].rearrange("p (c u e) -> p u c e", u=2, e=2), op=ALU.add)
+                nc.vector.tensor_tensor(out=part[m][:], in0=acc[m][:], in1=spread[n][:, 512 * m:512 * (m + 1)],
+                                        op=ALU.add)
 
         def larger(s):
             hs[s] = sb("hs", 512, BF16, 6)
+            big = sb("big", 512, BF16, 2)
             part = staged["part", s]
-            nc.vector.tensor_tensor(out=hs[s][:], in0=part[0][:], in1=part[1][:], op=ALU.max)
+            nc.vector.tensor_tensor(out=big[:], in0=part[0][:], in1=part[1][:], op=ALU.max)
+            nc.scalar.copy(out=hs[s][:].bitcast(F32).rearrange("p (u c) -> p u c", u=2),
+                           in_=big[:].bitcast(F32).rearrange("p (c u) -> p u c", u=2))
 
         def turn_h1(s, at):
             for j in range(4):
@@ -280,13 +299,13 @@ def tile_dialect_maxout_phoneme_scores_b12_kernel(
         def add_bias(i):
             zb[i] = sb("zb", NS, F32, 2)
             nc.vector.tensor_tensor(out=zb[i][:], in0=bank["z", i][:],
-                                    in1=s_bias[:, NS * (i // 2):NS * (i // 2 + 1)], op=ALU.add)
+                                    in1=score[i // 2][:, 0:NS], op=ALU.add)
 
         def gain(i):
             d, h = divmod(i, 2)
             yf[i] = sb("yf", NS, F32, 8)
             eng = nc.vector if GAIN[i] == "V" else nc.gpsimd
-            eng.tensor_tensor(out=yf[i][:], in0=zb[i][:], in1=s_gain[:, NS * d:NS * (d + 1)], op=ALU.mult)
+            eng.tensor_tensor(out=yf[i][:], in0=zb[i][:], in1=score[d][:, NS:2 * NS], op=ALU.mult)
             nc.sync.dma_start(out=out_0[d, P * h:P * (h + 1), :], in_=yf[i][:])
 
         def round_y(i):
@@ -321,15 +340,18 @@ def tile_dialect_maxout_phoneme_scores_b12_kernel(
         for i in range(2):
             widen(i, 0)
             widen(i, 1)
+        bt = psum.tile([P, 1024], BF16, name="h1", tag="h1")
         turn_x(0)
         exit_x(0)
-        quant_x(0)
         turn_x(1)
         exit_x(1)
-        bt = psum.tile([P, 1024], BF16, name="h1", tag="h1")
         nc.tensor.transpose(bt[:, 0:P], bias_rows[:], ident_b[:])
         nc.scalar.copy(out=bias_cols[:], in_=bt[:, 0:96])
+        sp = [spread_rows("h2", 1, 96, 112), spread_rows("acc1", 2, 100, 116)]
+        quant_x(0)
         quant_x(1)
+        for d in range(2):
+            copy_out(SPX[d], score[d][:], sp[d][:])
         nc.vector.memset(r_scales[:].bitcast(I32), 0)
         nc.vector.memset(wsr[0][:].bitcast(I32), 0)
         nc.vector.memset(wsr[1][:].bitcast(I32), 0)
@@ -337,20 +359,14 @@ def tile_dialect_maxout_phoneme_scores_b12_kernel(
         load_scales(ws1[1], V_scales[KP:2 * KP], F)
         load_w(0, 1)
         load_w(1, 1)
-        for n in range(3, 6):
-            load_spread(n)
         load_x(2)
         load_scales(r_scales, R_scales, NS)
         load_r(0)
-        nc.sync.dma_start(out=s_bias[:], in_=score_bias.rearrange("d n -> (d n)").partition_broadcast(P))
-        nc.sync.dma_start(out=s_gain[:], in_=score_gain.rearrange("d n -> (d n)").partition_broadcast(P))
         load_scales(wsr[0], U_scales[2 * KP:], F)
         load_scales(wsr[1], V_scales[2 * KP:], F)
         for d in range(2, G):
             load_w(0, d)
             load_w(1, d)
-            for n in range(FP * d, FP * (d + 1)):
-                load_spread(n)
             if d + 1 < G:
                 load_x(d + 1)
             load_r(d - 1)
@@ -369,7 +385,7 @@ def tile_dialect_maxout_phoneme_scores_b12_kernel(
                 fn(*args)
 
         def is_run(step):
-            return step >= last or step % RUN == RUN - 1
+            return step >= TAIL or step % RUN == RUN - 1
 
         def run_from(step):
             while not is_run(step):
@@ -385,7 +401,13 @@ def tile_dialect_maxout_phoneme_scores_b12_kernel(
             at(r, "turn", turn_x, i)
             at(r, "exit", exit_x, i)
             at(r + 1, "early", quant_x, i)
+        for n in NEED:
+            s = min(s for s, (d, h, g) in enumerate(UNITS) if FP * d + g == n and MODES[s] == "B")
+            at(max(s - SLEAD, 0), "pre", spread_unit, n)
+        at(SC2, "pre", spread_score, 2)
+        at(SC3, "pre", spread_score, 3)
         for s in range(last + 12):
+            run(s, "pre")
             if s <= last:
                 stage1(s)
             run(s, "mx")
@@ -393,7 +415,7 @@ def tile_dialect_maxout_phoneme_scores_b12_kernel(
             if s <= last:
                 maxout(s)
                 if MODES[s] == "C":
-                    wait1.append((s, s + LAG1 - (s >= last)))
+                    wait1.append((s, s + (LAG1 if s < TAIL else 1)))
                 elif s < last:
                     at(s + 1, "early", larger, s)
                     wait2.append((s, s + LAGB - (s + 1 >= last)))
@@ -423,12 +445,14 @@ def tile_dialect_maxout_phoneme_scores_b12_kernel(
                     i = 2 * UNITS[u][0] + UNITS[u][1]
                     left[i] = left[i] - 1
                     if left[i] == 0:
-                        z = s + 1 + (ZLAG if s < last else 1)
+                        z = s + 1 + (ZLAG if s < TAIL else ZT)
                         at(z, "mx", stage2, i, list(range(FP)))
                         at(z, "late", add_bias, i)
                         at(z + 1, "early", gain, i)
                         at(z + 1, "late", round_y, i)
-                        r = run_from(z + (YLAG if z + YLAG <= last else 1))
+                        r = run_from(z + (YLAG if z < TAIL else YT))
+                        while len(todo.get((r, "turn"), [])) >= YCAP:
+                            r = run_from(r + 1)
                         at(r, "turn", turn_y, i)
                         at(r, "exit", exit_y, i)
                         at(r + 1, "early", quant_y, i)

from contextlib import ExitStack

import concourse.mybir as mybir
from concourse.masks import make_identity

G, T, K, F, NS = 4, 256, 1024, 1536, 512
FLOPS = 2 * G * T * (2 * K * F + F * NS)

F32 = mybir.dt.float32
BF16 = mybir.dt.bfloat16
I32 = mybir.dt.int32
U32 = mybir.dt.uint32
U8 = mybir.dt.uint8
FP8 = mybir.dt.float8_e4m3fn
FP8X4 = mybir.dt.float8_e4m3fn_x4
FP4X4 = mybir.dt.float4_e2m1fn_x4
ALU = mybir.AluOpType
ACT = mybir.ActivationFunctionType

P = 128
KP = K // 512
FP = F // 512
NCH = G * FP
MODES = "C" * 24
WIDEN = "V" * 8
GAIN = "VVVVVVVV"
LAG1 = 2
LAG2 = 4
LAGB = 2
RUN = 2
XLEAD = 4
WLEAD = 3
ZLAG = 2
TAIL = 22
ZT = 1
YT = 2
SC2 = 2
SC3 = 4
YCAP = 2
SPX = "VSSS"
SLEAD = 2
YLAG = 3
UNITS = ([(0, h, g) for g in range(FP) for h in range(2)]
         + [(d, h, g) for d in range(1, G) for h in range(2) for g in range(FP)])
NEED = sorted(set(FP * d + g for i, (d, h, g) in enumerate(UNITS) if MODES[i] == "B"))


def tile_dialect_maxout_phoneme_scores_b12_kernel(
    tc, X_bytes, X_scale, U_words, U_scales, V_words, V_scales, R_words, R_scales,
    u_bias, v_bias, score_bias, score_gain, out_0, out_1, out_2,
):
    nc = tc.nc
    with ExitStack() as ctx:
        keep = ctx.enter_context(tc.tile_pool(name="keep", bufs=1))
        work = ctx.enter_context(tc.tile_pool(name="work", bufs=2))
        psum = ctx.enter_context(tc.psum_pool(name="psum", bufs=1))
        ctx.enter_context(tc.manual_schedule())

        def kept(name, shape, dtype):
            return keep.tile(shape, dtype, name=name, align_bytes=64)

        ident_f = kept("ident_f", [P, P], F32)
        ident_b = kept("ident_b", [P, P], BF16)
        bias_rows = kept("bias_rows", [P, P], BF16)
        bias_cols = kept("bias_cols", [P, 96], F32)
        warm = kept("warm", [P, 8], F32)
        x_scale = kept("x_scale", [P, 2 * G, 8], F32)
        x_bytes = [kept("x_bytes%d" % d, [P, 2, K], U8) for d in range(G)]
        w0 = [[kept("w0_%d_%d" % (m, g), [P, KP, 1024], U8) for g in range(FP)] for m in range(2)]
        wd = [[None] + [kept("w%d_%d" % (d, m), [P, KP, 2 * F], U8) for d in range(1, G)] for m in range(2)]
        ws0 = [kept("ws0_%d" % m, [P, KP * F], U8) for m in range(2)]
        ws1 = [kept("ws1_%d" % m, [P, KP * F], U8) for m in range(2)]
        wsr = [kept("wsr_%d" % m, [P, 2 * KP * F], U8) for m in range(2)]
        spread = {}
        r_words = [kept("r_words%d" % d, [P, FP, 2 * NS], U8) for d in range(G)]
        r_scales = kept("r_scales", [P, G * FP * NS], U8)
        score = [kept("score%d" % d, [P, 2 * NS], BF16) for d in range(G)]
        y_scales = [kept("y_scales%d" % i, [P, w], U8) for i, w in enumerate((7 * P, P))]
        y_words = [kept("y_words%d" % i, [P, T], U32) for i in range(G)]
        words_in = (U_words, V_words)
        scales_in = (U_scales, V_scales)

        def load_scales(tile, src, n):
            rows = src.rearrange("g (q r) n -> r q g n", r=4)
            for r in range(4):
                nc.sync.dma_start(
                    out=tile[r:P:32, :].bitcast(I32).rearrange("q (g n) -> q g n", n=n // 4),
                    in_=rows[r].bitcast(I32))

        def load_x(d):
            nc.sync.dma_start(out=x_bytes[d][:], in_=X_bytes[d].rearrange("(h p) k -> p h k", p=P))

        def load_w0(m, g):
            src = words_in[m][0:KP].rearrange("g p n -> p g n")[:, :, 1024 * g:1024 * (g + 1)]
            nc.sync.dma_start(out=w0[m][g][:].bitcast(I32), in_=src.bitcast(I32))

        def load_w(m, d):
            src = words_in[m][KP * d:KP * (d + 1)].rearrange("g p n -> p g n")
            nc.sync.dma_start(out=wd[m][d][:].bitcast(I32), in_=src.bitcast(I32))

        def load_r(d):
            src = R_words[FP * d:FP * (d + 1)].rearrange("g p n -> p g n")
            nc.sync.dma_start(out=r_words[d][:].bitcast(I32), in_=src.bitcast(I32))

        def w_operand(m, d, g, kp, c0, width):
            col = 512 * g + c0
            if d == 0:
                words = w0[m][g][:, kp, 2 * c0:2 * (c0 + width)]
            else:
                words = wd[m][d][:, kp, 2 * col:2 * (col + width)]
            plane = (ws0, ws1, wsr, wsr)[d][m]
            at = (max(d - 2, 0) * KP + kp) * F + col
            return words.bitcast(FP4X4), plane[:, at:at + width]

        nc.vector.memset(ws0[0][:].bitcast(I32), 0)
        nc.vector.memset(ws0[1][:].bitcast(I32), 0)
        nc.vector.memset(warm[:], 0.0)
        nc.vector.memset(ws1[0][:].bitcast(I32), 0)
        nc.vector.memset(ws1[1][:].bitcast(I32), 0)
        make_identity(nc, ident_f[:])
        make_identity(nc, ident_b[:])
        load_x(0)
        nc.sync.dma_start(out=x_scale[:], in_=X_scale.rearrange("d (h p) j -> p (d h) j", p=P))
        nc.scalar.dma_start(out=bias_rows[0:48, :], in_=u_bias.rearrange("d (j c) -> (d j) c", c=P))
        nc.scalar.dma_start(out=bias_rows[48:96, :], in_=v_bias.rearrange("d (j c) -> (d j) c", c=P))
        nc.scalar.dma_start(out=bias_rows[96:112, :], in_=score_bias.rearrange("d (j c) -> (d j) c", c=P))
        nc.scalar.dma_start(out=bias_rows[112:P, :], in_=score_gain.rearrange("d (j c) -> (d j) c", c=P))
        nc.scalar.activation(out=warm[:], in_=warm[:], func=ACT.Identity)
        load_w0(0, 0)
        load_scales(ws0[0], U_scales[0:KP], F)
        load_w0(1, 0)
        load_scales(ws0[1], V_scales[0:KP], F)
        for g in range(1, FP):
            load_w0(0, g)
            load_w0(1, g)
        load_x(1)

        xw, xq, xs, hn, hs, hq, hsc, yf, yb, zb = {}, {}, {}, {}, {}, {}, {}, {}, {}, {}
        bank, staged = {}, {}
        done = set()

        def aux():
            return psum.tile([P, 512], F32, name="aux", tag="aux", bufs=2)

        def sb(name, cols, dtype, bufs):
            return work.tile([P, cols], dtype, name=name, tag=name, bufs=bufs, align_bytes=64)

        def widen(i, part):
            d, h = divmod(i, 2)
            if part == 0:
                xw[i] = sb("xw", K, BF16, 2)
                if WIDEN[i] == "S":
                    staged["plain"] = sb("x_plain", K, BF16, 2)
            t = xw[i]
            if WIDEN[i] == "S":
                plain = staged["plain"]
                for blk in range(4 * part, 4 * part + 4):
                    nc.scalar.activation(out=plain[:, P * blk:P * (blk + 1)], func=ACT.Copy,
                                         in_=x_bytes[d][:, h, P * blk:P * (blk + 1)].bitcast(FP8),
                                         scale=x_scale[:, i, blk:blk + 1])
                cols = slice(512 * part, 512 * (part + 1))
                nc.scalar.copy(out=t[:, cols].bitcast(F32).rearrange("p (u c) -> p u c", u=2),
                               in_=plain[:, cols].bitcast(F32).rearrange("p (c u) -> p u c", u=2))
                return
            dst = t[:].rearrange("p (g u b a e) -> p g b a u e", g=KP, u=2, b=4, e=2)
            for blk in range(4 * part, 4 * part + 4):
                src = x_bytes[d][:, h, P * blk:P * (blk + 1)].bitcast(FP8)
                nc.vector.tensor_scalar(
                    out=dst[:, blk // 4, blk % 4], in0=src.rearrange("p (a u e) -> p a u e", u=2, e=2),
                    scalar1=x_scale[:, i, blk:blk + 1], scalar2=None, op0=ALU.mult)

        def turn_words(dst, src):
            words = src.bitcast(F32)
            for i in range(words.shape[1] // P):
                nc.tensor.transpose(dst[:, P * i:P * (i + 1)], words[:, P * i:P * (i + 1)], ident_f[:])

        def interleave_out(name, src, bufs):
            t = sb(name, 2 * src.shape[1], BF16, bufs)
            nc.scalar.copy(out=t[:].bitcast(F32).rearrange("p (i c u) -> p i c u", c=P, u=2),
                           in_=src.rearrange("p (i u c) -> p i c u", c=P, u=2))
            return t

        def quant(src, codes, scales):
            nc.vector.quantize_mx(out=codes.bitcast(FP8X4), scales=scales, in_=src[:])

        def spread_rows(tag, bufs, first, second):
            b = psum.tile([P, 1024], BF16, name=tag, tag=tag, bufs=bufs)
            for k, r in enumerate(list(range(first, first + 4)) + list(range(second, second + 4))):
                nc.tensor.matmul(b[:, P * k:P * (k + 1)], lhsT=ident_b[:, r:r + 1].to_broadcast([P, P]),
                                 rhs=bias_rows[:], start=True, stop=True)
            return b

        def copy_out(which, dst, src):
            if which == "S":
                nc.scalar.copy(out=dst, in_=src)
            else:
                nc.vector.tensor_copy(out=dst, in_=src)

        def spread_unit(n):
            b = spread_rows("aux", 2, 4 * n, 48 + 4 * n)
            spread[n] = sb("spread", 1024, BF16, 4)
            nc.scalar.copy(out=spread[n][:], in_=b[:])

        def spread_score(d):
            copy_out(SPX[d], score[d][:], spread_rows("aux", 2, 96 + 4 * d, 112 + 4 * d)[:])

        def turn_x(i):
            bank["x", i] = aux()
            turn_words(bank["x", i], xw[i][:])

        def exit_x(i):
            staged["x", i] = interleave_out("x_in", bank["x", i][:], 2)

        def quant_x(i):
            xq[i] = sb("xq", KP * P, U32, 4)
            xs[i] = sb("xs", KP * P, U8, 4)
            quant(staged["x", i], xq[i][:], xs[i][:])

        def stage1(s):
            d, h, g = UNITS[s]
            i = 2 * d + h
            n = FP * d + g
            acc = []
            for m in range(2):
                b = psum.tile([P, 512], F32, name="acc%d" % m, tag="acc%d" % m, bufs=2)
                acc.append(b)
                for j in range(4 if MODES[s] == "C" else 1):
                    for kp in range(KP):
                        xc = xq[i][:, P * kp:P * (kp + 1)].bitcast(FP8X4)
                        xp = xs[i][:, P * kp:P * (kp + 1)]
                        if MODES[s] == "C":
                            ww, wsc = w_operand(m, d, g, kp, P * j, P)
                            nc.tensor.matmul_mx(out=b[:, P * j:P * (j + 1)], lhsT=ww, lhsT_scale=wsc, rhs=xc,
                                                rhs_scale=xp, start=(kp == 0), stop=(kp == KP - 1))
                        else:
                            ww, wsc = w_operand(m, d, g, kp, 0, 512)
                            nc.tensor.matmul_mx(out=b[:], lhsT=xc, lhsT_scale=xp, rhs=ww, rhs_scale=wsc,
                                                start=(kp == 0), stop=(kp == KP - 1))
            bank["acc", s] = acc

        def maxout(s):
            d, h, g = UNITS[s]
            n = FP * d + g
            acc = bank["acc", s]
            if MODES[s] == "C":
                hn[s] = sb("hn", 512, BF16, 4)
                tmp = [sb("a_tmp", P, F32, 8) for j in range(4)]
                for j in range(4):
                    nc.scalar.activation(out=tmp[j][:], in_=acc[0][:, P * j:P * (j + 1)], func=ACT.Identity,
                                         bias=bias_cols[:, 4 * n + j:4 * n + j + 1])
                for j in range(4):
                    nc.vector.scalar_tensor_tensor(
                        out=hn[s][:, P * j:P * (j + 1)], in0=acc[1][:, P * j:P * (j + 1)],
                        scalar=bias_cols[:, 48 + 4 * n + j:49 + 4 * n + j], in1=tmp[j][:], op0=ALU.add, op1=ALU.max)
                return
            part = [sb("part", 512, BF16, 4) for m in range(2)]
            staged["part", s] = part
            for m in range(2):
                nc.vector.tensor_tensor(out=part[m][:], in0=acc[m][:], in1=spread[n][:, 512 * m:512 * (m + 1)],
                                        op=ALU.add)

        def larger(s):
            hs[s] = sb("hs", 512, BF16, 6)
            big = sb("big", 512, BF16, 2)
            part = staged["part", s]
            nc.vector.tensor_tensor(out=big[:], in0=part[0][:], in1=part[1][:], op=ALU.max)
            nc.scalar.copy(out=hs[s][:].bitcast(F32).rearrange("p (u c) -> p u c", u=2),
                           in_=big[:].bitcast(F32).rearrange("p (c u) -> p u c", u=2))

        def turn_h1(s, at):
            for j in range(4):
                nc.tensor.transpose(bank["h1"][:, 512 * at + P * j:512 * at + P * (j + 1)],
                                    hn[s][:, P * j:P * (j + 1)], ident_b[:])

        def exit_h1(s, at):
            hs[s] = sb("hs", 512, BF16, 6)
            nc.scalar.copy(out=hs[s][:].bitcast(F32).rearrange("p (u c) -> p u c", u=2),
                           in_=bank["h1"][:, 512 * at:512 * (at + 1)].bitcast(F32).rearrange("p (c u) -> p u c", u=2))

        def quant_h(group):
            src = staged["h"]
            codes = sb("hq", P * len(group), U32, 5)
            plane = sb("hsc", P * len(group), U8, 5)
            quant(src, codes[:], plane[:])
            for at, s in enumerate(group):
                hq[UNITS[s]] = (codes[:, P * at:P * (at + 1)].bitcast(FP8X4), plane[:, P * at:P * (at + 1)])

        def stage2(i, passes):
            d, h = divmod(i, 2)
            if passes[0] == 0:
                bank["z", i] = aux()
            for g in passes:
                n = FP * d + g
                nc.tensor.matmul_mx(
                    out=bank["z", i][:], lhsT=hq[d, h, g][0], lhsT_scale=hq[d, h, g][1],
                    rhs=r_words[d][:, g, :].bitcast(FP4X4), rhs_scale=r_scales[:, NS * n:NS * (n + 1)],
                    start=(g == 0), stop=(g == FP - 1))

        def add_bias(i):
            zb[i] = sb("zb", NS, F32, 2)
            nc.vector.tensor_tensor(out=zb[i][:], in0=bank["z", i][:],
                                    in1=score[i // 2][:, 0:NS], op=ALU.add)

        def gain(i):
            d, h = divmod(i, 2)
            yf[i] = sb("yf", NS, F32, 8)
            eng = nc.vector if GAIN[i] == "V" else nc.gpsimd
            eng.tensor_tensor(out=yf[i][:], in0=zb[i][:], in1=score[d][:, NS:2 * NS], op=ALU.mult)
            nc.sync.dma_start(out=out_0[d, P * h:P * (h + 1), :], in_=yf[i][:])

        def round_y(i):
            yb[i] = sb("yb", NS, BF16, 2)
            nc.scalar.copy(out=yb[i][:].rearrange("p (u c e) -> p u c e", u=2, e=2),
                           in_=yf[i][:].rearrange("p (c u e) -> p u c e", u=2, e=2))

        def turn_y(i):
            bank["y", i] = aux()
            turn_words(bank["y", i], yb[i][:])

        def exit_y(i):
            staged["y", i] = interleave_out("y_in", bank["y", i][:, 0:T], 2)

        def quant_y(i):
            d, h = divmod(i, 2)
            done.add(i)
            assert i < 6 or len(done) == i + 1
            quant(staged["y", i], y_words[d][:, P * h:P * (h + 1)], y_scales[i // 7][:, P * (i % 7):P * (i % 7 + 1)])
            rows = out_1[0].rearrange("p m t -> p (m t)").bitcast(I32)
            if i >= 6:
                nc.sync.dma_start(out=rows[:, P * i:P * (i + 1)], in_=y_words[d][:, P * h:P * (h + 1)].bitcast(I32))
            elif 2 * d + 1 - h in done:
                nc.sync.dma_start(out=rows[:, T * d:T * (d + 1)], in_=y_words[d][:].bitcast(I32))
            if i >= 6:
                cols = slice(0, 7 * P) if i == 6 else slice(7 * P, 8 * P)
                for q in range(4):
                    eng = nc.scalar if (i == 7 and q % 2) else nc.sync
                    eng.dma_start(out=out_2[0, 4 * q:4 * q + 4, cols].bitcast(I32),
                                  in_=y_scales[i // 7][32 * q:32 * q + 4, :].bitcast(I32))

        for i in range(2):
            widen(i, 0)
            widen(i, 1)
        bt = psum.tile([P, 1024], BF16, name="h1", tag="h1")
        turn_x(0)
        exit_x(0)
        turn_x(1)
        exit_x(1)
        nc.tensor.transpose(bt[:, 0:P], bias_rows[:], ident_b[:])
        nc.scalar.copy(out=bias_cols[:], in_=bt[:, 0:96])
        sp = [spread_rows("h2", 1, 96, 112), spread_rows("acc1", 2, 100, 116)]
        quant_x(0)
        quant_x(1)
        for d in range(2):
            copy_out(SPX[d], score[d][:], sp[d][:])
        nc.vector.memset(r_scales[:].bitcast(I32), 0)
        nc.vector.memset(wsr[0][:].bitcast(I32), 0)
        nc.vector.memset(wsr[1][:].bitcast(I32), 0)
        load_scales(ws1[0], U_scales[KP:2 * KP], F)
        load_scales(ws1[1], V_scales[KP:2 * KP], F)
        load_w(0, 1)
        load_w(1, 1)
        load_x(2)
        load_scales(r_scales, R_scales, NS)
        load_r(0)
        load_scales(wsr[0], U_scales[2 * KP:], F)
        load_scales(wsr[1], V_scales[2 * KP:], F)
        for d in range(2, G):
            load_w(0, d)
            load_w(1, d)
            if d + 1 < G:
                load_x(d + 1)
            load_r(d - 1)
        load_r(G - 1)


        last = len(UNITS) - 1
        start_of = {2 * d + h: min(s for s, u in enumerate(UNITS) if u[:2] == (d, h)) for d in range(G) for h in range(2)}
        todo = {}

        def at(step, slot, fn, *args):
            todo.setdefault((step, slot), []).append((fn, args))

        def run(step, slot):
            for fn, args in todo.get((step, slot), []):
                fn(*args)

        def is_run(step):
            return step >= TAIL or step % RUN == RUN - 1

        def run_from(step):
            while not is_run(step):
                step = step + 1
            return step

        wait1, wait2 = [], []
        left = {i: FP for i in range(2 * G)}
        for i in range(2, 2 * G):
            r = run_from(max(start_of[i] - XLEAD, 1))
            at(max(r - WLEAD, 0), "late", widen, i, 0)
            at(max(r - WLEAD, 0) + 1, "late", widen, i, 1)
            at(r, "turn", turn_x, i)
            at(r, "exit", exit_x, i)
            at(r + 1, "early", quant_x, i)
        for n in NEED:
            s = min(s for s, (d, h, g) in enumerate(UNITS) if FP * d + g == n and MODES[s] == "B")
            at(max(s - SLEAD, 0), "pre", spread_unit, n)
        at(SC2, "pre", spread_score, 2)
        at(SC3, "pre", spread_score, 3)
        for s in range(last + 12):
            run(s, "pre")
            if s <= last:
                stage1(s)
            run(s, "mx")
            run(s, "early")
            if s <= last:
                maxout(s)
                if MODES[s] == "C":
                    wait1.append((s, s + (LAG1 if s < TAIL else 1)))
                elif s < last:
                    at(s + 1, "early", larger, s)
                    wait2.append((s, s + LAGB - (s + 1 >= last)))
                else:
                    larger(s)
                    wait2.append((s, s + 1))
            run(s, "late")
            if not is_run(s):
                continue
            first = [u for u, due in wait1 if due <= s][:2]
            second = [u for u, due in sorted(wait2) if due <= s][:2]
            wait1 = [w for w in wait1 if w[0] not in first]
            wait2 = [w for w in wait2 if w[0] not in second]
            if second:
                bank["h2"] = psum.tile([P, 512], F32, name="h2", tag="h2")
                for k, u in enumerate(second):
                    turn_words(bank["h2"][:, T * k:T * (k + 1)], hs[u][:])
            run(s, "turn")
            if first:
                bank["h1"] = psum.tile([P, 1024], BF16, name="h1", tag="h1")
                for k, u in enumerate(first):
                    turn_h1(u, k)
            if second:
                staged["h"] = interleave_out("h_in", bank["h2"][:, 0:T * len(second)], 2)
                at(s + 1, "early", quant_h, second)
                for u in second:
                    i = 2 * UNITS[u][0] + UNITS[u][1]
                    left[i] = left[i] - 1
                    if left[i] == 0:
                        z = s + 1 + (ZLAG if s < TAIL else ZT)
                        at(z, "mx", stage2, i, list(range(FP)))
                        at(z, "late", add_bias, i)
                        at(z + 1, "early", gain, i)
                        at(z + 1, "late", round_y, i)
                        r = run_from(z + (YLAG if z < TAIL else YT))
                        while len(todo.get((r, "turn"), [])) >= YCAP:
                            r = run_from(r + 1)
                        at(r, "turn", turn_y, i)
                        at(r, "exit", exit_y, i)
                        at(r + 1, "early", quant_y, i)
            run(s, "exit")
            for k, u in enumerate(first):
                exit_h1(u, k)
                wait2.append((u, s + 1))
